import numpy as np
CORES = [2,6,26,30,66,70,74,78,82,86]
N = 10
TK = 512
D = 128 * N
EPS = 0.01
def setup_inputs(rng):
    return {"x": (rng.standard_normal((N, 128, TK), dtype=np.float32) * (0.5 + np.abs(rng.standard_normal((1, 1, TK), dtype=np.float32))) + rng.standard_normal((1, 1, TK), dtype=np.float32))}
def setup_inputs_big(rng):
    d = setup_inputs(rng)
    for k in ("x",): d[k] = (d[k].astype(np.float32) * 1048576.0).astype(d[k].dtype)
    return d
def setup_inputs_small(rng):
    d = setup_inputs(rng)
    for k in ("x",): d[k] = (d[k].astype(np.float32) * (1 / 1048576.0)).astype(d[k].dtype)
    return d
def setup_inputs_apart(rng):
    d = setup_inputs(rng)
    f = (10.0 ** rng.permutation(np.linspace(-1.5, 1.5, N))).astype(np.float32).reshape(N, 1, 1)
    for k in ("x",): d[k] = (d[k].astype(np.float32) * f).astype(d[k].dtype)
    return d
def setup_inputs_mixed(rng):
    d = setup_inputs(rng)
    f = (10.0 ** rng.uniform(-3, 3, (1, 1, TK))).astype(np.float32); shape = rng.integers(3, size=(1, 1, TK))
    for k in ("x",):
        x = d[k].astype(np.float32)
        m = x.mean(axis=(0, 1), keepdims=True); level = m + np.sign(x - m) * np.abs(x - m).mean(axis=(0, 1), keepdims=True) * rng.uniform(0.9, 1.1, x.shape).astype(np.float32)
        other = x * np.where(rng.random(x.shape) < 0.5, 0.1, 1.0).astype(np.float32)
        d[k] = (np.where(shape == 1, level, np.where(shape == 2, other, x)) * f).astype(d[k].dtype)
    return d
def reference(x):
    X = x.astype(np.float64)
    Z = X
    Z = Z / np.sqrt((Z ** 2).sum(axis=(0, 1)) / D + EPS)
    return {"y": Z.astype(np.float32)}

@@ -1,0 +1,148 @@
+from concourse.bass import DstId, RemoteDMATransfer
+from concourse.mybir import AluOpType, AxisListType, ActivationFunctionType
+
+N = 10
+TK = 512
+D = 128 * N
+EPS = 0.01
+NENG = 4
+
+SCRATCH = {
+    "xs": ("sbuf", [128, TK], "float32"),
+    "sqp": ("sbuf", [128, TK], "float32"),
+    "ys": ("sbuf", [128, TK], "float32"),
+    "ones32": ("sbuf", [128, 128], "float32"),
+    "ident": ("sbuf", [128, 128], "float32"),
+    "onesb": ("sbuf", [128, 128], "bfloat16"),
+    "jj": ("sbuf", [128, 64], "bfloat16"),
+    "sel": ("sbuf", [128, 8], "float32"),
+    "part": ("sbuf", [128, 4], "float32"),
+    "land": ("dram", [N, 128, 4], "float32"),
+    "gg": ("sbuf", [128, 128], "float32"),
+    "sd": ("sbuf", [128, 8], "float32"),
+    "rstd": ("sbuf", [128, 8], "float32"),
+    "hib": ("sbuf", [128, 8], "bfloat16"),
+    "w": ("sbuf", [128, 8], "float32"),
+    "dg": ("sbuf", [128, TK], "bfloat16"),
+    "ps_part": ("psum", [128, 512], "float32"),
+    "ps_a": ("psum", [128, 512], "float32"),
+    "b0": ("psum", [128, 512], "float32"),
+    "b1": ("psum", [128, 512], "float32"),
+    "b2": ("psum", [128, 512], "float32"),
+    "b3": ("psum", [128, 512], "float32"),
+}
+SEMAPHORES = (["c_ones", "c_id", "c_set", "ld", "mm", "pc", "d1", "sent", "arrived", "d2", "am", "sq_s", "r1", "h1",
+               "w1", "ym", "st"]
+              + ["sq%d" % j for j in range(4)] + ["bd%d" % c for c in range(8)] + ["bm%d" % k for k in range(4)])
+
+
+def _hops(topo, a, b):
+    ca, cb = topo.chip(a), topo.chip(b)
+    if ca == cb:
+        return 0
+    if topo.mates(ca, cb) or topo.same_plane(ca, cb):
+        return 1
+    return 2
+
+
+def rank_program(g, core, T, topo):
+    rank = T.rank_of(core)
+    if rank is None:
+        return
+    S = T.sem
+    AF = ActivationFunctionType
+    v, sc, pe, sy = g.vector, g.scalar, g.tensor, g.sync
+    bank = [T.b0, T.b1, T.b2, T.b3]
+
+    sy.dma_start(T.xs[:, :], T.x[:, :]).then_inc(S.ld, 16)
+
+    v.memset(T.ones32[:, :], 1.0).then_inc(S.c_ones, 1)
+    v.memset(T.onesb[:, :], 1.0).then_inc(S.c_set, 1)
+    g.wait_ge(S.c_ones, 1)
+    g.affine_select(T.ident[:, :], T.ones32[:, :], [[-1, 128]], AluOpType.is_equal, 0.0, 0, 1).then_inc(S.c_id, 1)
+    v.wait_ge(S.c_id, 1)
+    v.tensor_tensor(T.jj[:, :], T.ident[:, 0:64], T.ident[:, 64:128], AluOpType.add).then_inc(S.c_set, 1)
+    for c in range(8):
+        v.tensor_reduce(T.sel[:, c:c + 1], T.ident[:, c:128:8], AxisListType.X, AluOpType.add).then_inc(S.c_set, 1)
+    n_set = 10
+
+    sc.wait_ge(S.ld, 16)
+    for j in range(4):
+        sc.activation(T.sqp[:, 128 * j:128 * (j + 1)], T.xs[:, j:TK:4], AF.Square).then_inc(S["sq%d" % j], 1)
+    pe.wait_ge(S.c_ones, 1)
+    for j in range(4):
+        pe.wait_ge(S["sq%d" % j], 1)
+        pe.matmul(T.ps_part[:, j:j + 1], T.sqp[:, 128 * j:128 * (j + 1)], T.ones32[:, 0:1], True, True).then_inc(S.mm, 1)
+    v.wait_ge(S.mm, 4)
+    v.tensor_copy(T.part[:, :], T.ps_part[:, 0:4]).then_inc(S.pc, 1)
+
+    sy.wait_ge(S.pc, 1)
+    sy.dma_start(T.land[rank], T.part[:, :]).then_inc(S.d1, 16)
+
+    others = [c for c in T.cores if c != core]
+    common = 0xFFFF
+    for c in others:
+        assert topo.may_write(core, c)
+        common &= topo.mask(core, c)
+    bits = [b for b in range(16) if (common >> b) & 1]
+    engines = bits[::2][:NENG]
+    others.sort(key=lambda c: -_hops(topo, core, c))
+    transfers = []
+    for e, b in enumerate(engines):
+        mine = others[e::len(engines)]
+        ids = []
+        for c in mine:
+            rid, pid, _se = topo.addr(c)
+            ids.append(DstId(rid=rid, pnc=pid))
+        transfers.append(RemoteDMATransfer(dst_ids=ids, dma_engine_mask=1 << b, remote_sem=S.arrived,
+                                           srcs=[T.land[rank]], dsts=[T.land[rank] for _c in mine]))
+    g.wait_ge(S.d1, 16)
+    g.remote_dma_fused(transfers, local_sem=S.sent)
+
+    sy.wait_ge(S.d1, 16)
+    sy.wait_ge(S.arrived, N - 1)
+    sy.dma_start(T.gg[0:8 * N, 0:64], T.land[:]).then_inc(S.d2, 16)
+    sc.wait_ge(S.d1, 16)
+    sc.wait_ge(S.arrived, N - 1)
+    sc.dma_start(T.gg[0:8 * N, 64:128], T.land[:]).then_inc(S.d2, 16)
+
+    pe.wait_ge(S.c_set, n_set)
+    pe.wait_ge(S.d2, 32)
+    pe.matmul(T.ps_a[:, 0:8], T.gg[0:8 * N, :], T.sel[0:8 * N, :], True, True).then_inc(S.am, 1)
+
+    sc.wait_ge(S.am, 1)
+    sc.activation(T.sd[:, :], T.ps_a[:, 0:8], AF.Sqrt, bias=EPS, scale=1.0 / D).then_inc(S.sq_s, 1)
+    v.wait_ge(S.sq_s, 1)
+    v.reciprocal(T.rstd[:, :], T.sd[:, :]).then_inc(S.r1, 1)
+    v.wait_ge(S.r1, 1)
+    v.tensor_copy(T.hib[:, :], T.rstd[:, :]).then_inc(S.h1, 1)
+    v.wait_ge(S.h1, 1)
+    v.tensor_tensor(T.w[64:128, :], T.rstd[64:128, :], T.hib[64:128, :], AluOpType.subtract).then_inc(S.w1, 1)
+    sc.wait_ge(S.h1, 1)
+    sc.activation(T.w[0:64, :], T.hib[0:64, :], AF.Copy).then_inc(S.w1, 1)
+
+    v.wait_ge(S.c_set, n_set)
+    v.wait_ge(S.w1, 2)
+    sc.wait_ge(S.c_set, n_set)
+    sc.wait_ge(S.w1, 2)
+    for c in range(8):
+        blk = T.dg[:, 64 * c:64 * (c + 1)]
+        if c % 2 == 0:
+            v.tensor_scalar(blk, T.jj[:, :], T.w[:, c:c + 1], None, AluOpType.mult).then_inc(S["bd%d" % c], 1)
+        else:
+            sc.activation(blk, T.jj[:, :], AF.Copy, scale=T.w[:, c:c + 1]).then_inc(S["bd%d" % c], 1)
+    for c in range(8):
+        pe.wait_ge(S["bd%d" % c], 1)
+        h = 64 * (c % 2)
+        pe.matmul(bank[c // 2][:, h:h + 64], T.onesb[:, :], T.dg[:, 64 * c:64 * (c + 1)], True, True).then_inc(
+            S["bm%d" % (c // 2)], 1)
+
+    v.wait_ge(S.ld, 16)
+    for k in range(4):
+        v.wait_ge(S["bm%d" % k], 2)
+        v.tensor_tensor(T.ys[:, 128 * k:128 * (k + 1)], T.xs[:, 128 * k:128 * (k + 1)], bank[k][:, 0:128],
+                        AluOpType.mult).then_inc(S.ym, 1)
+    sy.wait_ge(S.ym, 4)
+    sy.dma_start(T.y[:, :], T.ys[:, :]).then_inc(S.st, 16)
+    sy.wait_ge(S.st, 16)
+    g.wait_ge(S.sent, len(engines))

@@ -6,6 +6,8 @@ TK = 512
 D = 128 * N
 EPS = 0.01
 NENG = 4
+FIRST = (0, 128)
+NB = (1, 3)
 
 SCRATCH = {
     "xs": ("sbuf", [128, TK], "float32"),
@@ -16,23 +18,27 @@ SCRATCH = {
     "onesb": ("sbuf", [128, 128], "bfloat16"),
     "jj": ("sbuf", [128, 64], "bfloat16"),
     "sel": ("sbuf", [128, 8], "float32"),
-    "part": ("sbuf", [128, 4], "float32"),
-    "land": ("dram", [N, 128, 4], "float32"),
-    "gg": ("sbuf", [128, 128], "float32"),
+    "part": ("sbuf", [128, 8], "float32"),
+    "land0": ("dram", [N, 128, NB[0]], "float32"),
+    "land1": ("dram", [N, 128, NB[1]], "float32"),
+    "gg0": ("sbuf", [128, 128], "float32"),
+    "gg1": ("sbuf", [128, 128], "float32"),
     "sd": ("sbuf", [128, 8], "float32"),
     "rstd": ("sbuf", [128, 8], "float32"),
     "hib": ("sbuf", [128, 8], "bfloat16"),
     "w": ("sbuf", [128, 8], "float32"),
     "dg": ("sbuf", [128, TK], "bfloat16"),
-    "ps_part": ("psum", [128, 512], "float32"),
-    "ps_a": ("psum", [128, 512], "float32"),
+    "ps_p0": ("psum", [128, 512], "float32"),
+    "ps_p1": ("psum", [128, 512], "float32"),
+    "ps_a0": ("psum", [128, 512], "float32"),
+    "ps_a1": ("psum", [128, 512], "float32"),
     "b0": ("psum", [128, 512], "float32"),
     "b1": ("psum", [128, 512], "float32"),
     "b2": ("psum", [128, 512], "float32"),
     "b3": ("psum", [128, 512], "float32"),
 }
-SEMAPHORES = (["c_ones", "c_id", "c_set", "ld", "mm", "pc", "d1", "sent", "arrived", "d2", "am", "sq_s", "r1", "h1",
-               "w1", "ym", "st"]
+SEMAPHORES = (["c_ones", "c_id", "c_set", "sent", "r1", "h1", "w1", "ym", "st"]
+              + [n + "%d" % h for h in range(2) for n in ("ld", "mm", "pc", "d1", "arr", "d2", "am", "ss")]
               + ["sq%d" % j for j in range(4)] + ["bd%d" % c for c in range(8)] + ["bm%d" % k for k in range(4)])
 
 
@@ -53,8 +59,16 @@ def rank_program(g, core, T, topo):
     AF = ActivationFunctionType
     v, sc, pe, sy = g.vector, g.scalar, g.tensor, g.sync
     bank = [T.b0, T.b1, T.b2, T.b3]
+    ps_p = [T.ps_p0, T.ps_p1]
+    ps_a = [T.ps_a0, T.ps_a1]
+    land = [T.land0, T.land1]
+    gg = [T.gg0, T.gg1]
+    end = [FIRST[h] + 128 * NB[h] for h in range(2)]
+    col = [FIRST[h] // 64 for h in range(2)]
+    rows = [2 * NB[h] * N for h in range(2)]
 
-    sy.dma_start(T.xs[:, :], T.x[:, :]).then_inc(S.ld, 16)
+    for h in range(2):
+        sy.dma_start(T.xs[:, FIRST[h]:end[h]], T.x[:, FIRST[h]:end[h]]).then_inc(S["ld%d" % h], 16)
 
     v.memset(T.ones32[:, :], 1.0).then_inc(S.c_ones, 1)
     v.memset(T.onesb[:, :], 1.0).then_inc(S.c_set, 1)
@@ -62,22 +76,11 @@ def rank_program(g, core, T, topo):
     g.affine_select(T.ident[:, :], T.ones32[:, :], [[-1, 128]], AluOpType.is_equal, 0.0, 0, 1).then_inc(S.c_id, 1)
     v.wait_ge(S.c_id, 1)
     v.tensor_tensor(T.jj[:, :], T.ident[:, 0:64], T.ident[:, 64:128], AluOpType.add).then_inc(S.c_set, 1)
-    for c in range(8):
-        v.tensor_reduce(T.sel[:, c:c + 1], T.ident[:, c:128:8], AxisListType.X, AluOpType.add).then_inc(S.c_set, 1)
+    for h in range(2):
+        for b in range(2 * NB[h]):
+            v.tensor_reduce(T.sel[:, col[h] + b:col[h] + b + 1], T.ident[:, b:rows[h]:2 * NB[h]], AxisListType.X,
+                            AluOpType.add).then_inc(S.c_set, 1)
     n_set = 10
-
-    sc.wait_ge(S.ld, 16)
-    for j in range(4):
-        sc.activation(T.sqp[:, 128 * j:128 * (j + 1)], T.xs[:, j:TK:4], AF.Square).then_inc(S["sq%d" % j], 1)
-    pe.wait_ge(S.c_ones, 1)
-    for j in range(4):
-        pe.wait_ge(S["sq%d" % j], 1)
-        pe.matmul(T.ps_part[:, j:j + 1], T.sqp[:, 128 * j:128 * (j + 1)], T.ones32[:, 0:1], True, True).then_inc(S.mm, 1)
-    v.wait_ge(S.mm, 4)
-    v.tensor_copy(T.part[:, :], T.ps_part[:, 0:4]).then_inc(S.pc, 1)
-
-    sy.wait_ge(S.pc, 1)
-    sy.dma_start(T.land[rank], T.part[:, :]).then_inc(S.d1, 16)
 
     others = [c for c in T.cores if c != core]
     common = 0xFFFF
@@ -87,32 +90,55 @@ def rank_program(g, core, T, topo):
     bits = [b for b in range(16) if (common >> b) & 1]
     engines = bits[::2][:NENG]
     others.sort(key=lambda c: -_hops(topo, core, c))
-    transfers = []
-    for e, b in enumerate(engines):
-        mine = others[e::len(engines)]
-        ids = []
-        for c in mine:
-            rid, pid, _se = topo.addr(c)
-            ids.append(DstId(rid=rid, pnc=pid))
-        transfers.append(RemoteDMATransfer(dst_ids=ids, dma_engine_mask=1 << b, remote_sem=S.arrived,
-                                           srcs=[T.land[rank]], dsts=[T.land[rank] for _c in mine]))
-    g.wait_ge(S.d1, 16)
-    g.remote_dma_fused(transfers, local_sem=S.sent)
 
-    sy.wait_ge(S.d1, 16)
-    sy.wait_ge(S.arrived, N - 1)
-    sy.dma_start(T.gg[0:8 * N, 0:64], T.land[:]).then_inc(S.d2, 16)
-    sc.wait_ge(S.d1, 16)
-    sc.wait_ge(S.arrived, N - 1)
-    sc.dma_start(T.gg[0:8 * N, 64:128], T.land[:]).then_inc(S.d2, 16)
+    def gather_call(slot, sem):
+        transfers = []
+        for e, b in enumerate(engines):
+            mine = others[e::len(engines)]
+            ids = []
+            for c in mine:
+                rid, pid, _se = topo.addr(c)
+                ids.append(DstId(rid=rid, pnc=pid))
+            transfers.append(RemoteDMATransfer(dst_ids=ids, dma_engine_mask=1 << b, remote_sem=sem,
+                                               srcs=[slot], dsts=[slot for _c in mine]))
+        g.remote_dma_fused(transfers, local_sem=S.sent)
+
+    pe.wait_ge(S.c_ones, 1)
+    for h in range(2):
+        sc.wait_ge(S["ld%d" % h], 16)
+        for j in range(NB[h]):
+            q = FIRST[h] // 128 + j
+            sc.activation(T.sqp[:, 128 * q:128 * (q + 1)], T.xs[:, FIRST[h] + j:end[h]:NB[h]], AF.Square).then_inc(
+                S["sq%d" % q], 1)
+            pe.wait_ge(S["sq%d" % q], 1)
+            pe.matmul(ps_p[h][:, j:j + 1], T.sqp[:, 128 * q:128 * (q + 1)], T.ones32[:, 0:1], True, True).then_inc(
+                S["mm%d" % h], 1)
+        v.wait_ge(S["mm%d" % h], NB[h])
+        v.tensor_copy(T.part[:, 4 * h:4 * h + NB[h]], ps_p[h][:, 0:NB[h]]).then_inc(S["pc%d" % h], 1)
+        sy.wait_ge(S["pc%d" % h], 1)
+        sy.dma_start(land[h][rank], T.part[:, 4 * h:4 * h + NB[h]]).then_inc(S["d1%d" % h], 16)
+        g.wait_ge(S["d1%d" % h], 16)
+        gather_call(land[h][rank], S["arr%d" % h])
+
+    for h, queues in ((0, (sy, sc)), (1, (sy, sy))):
+        for i, q in enumerate(queues):
+            if i == 0 or q is not queues[0]:
+                q.wait_ge(S["d1%d" % h], 16)
+                q.wait_ge(S["arr%d" % h], N - 1)
+            q.dma_start(gg[h][0:rows[h], 64 * i:64 * (i + 1)], land[h][:]).then_inc(S["d2%d" % h], 16)
 
     pe.wait_ge(S.c_set, n_set)
-    pe.wait_ge(S.d2, 32)
-    pe.matmul(T.ps_a[:, 0:8], T.gg[0:8 * N, :], T.sel[0:8 * N, :], True, True).then_inc(S.am, 1)
+    for h in range(2):
+        pe.wait_ge(S["d2%d" % h], 32)
+        pe.matmul(ps_a[h][:, 0:2 * NB[h]], gg[h][0:rows[h], :], T.sel[0:rows[h], col[h]:col[h] + 2 * NB[h]], True,
+                  True).then_inc(S["am%d" % h], 1)
 
-    sc.wait_ge(S.am, 1)
-    sc.activation(T.sd[:, :], T.ps_a[:, 0:8], AF.Sqrt, bias=EPS, scale=1.0 / D).then_inc(S.sq_s, 1)
-    v.wait_ge(S.sq_s, 1)
+    for h in range(2):
+        sc.wait_ge(S["am%d" % h], 1)
+        sc.activation(T.sd[:, col[h]:col[h] + 2 * NB[h]], ps_a[h][:, 0:2 * NB[h]], AF.Sqrt, bias=EPS,
+                      scale=1.0 / D).then_inc(S["ss%d" % h], 1)
+    v.wait_ge(S.ss0, 1)
+    v.wait_ge(S.ss1, 1)
     v.reciprocal(T.rstd[:, :], T.sd[:, :]).then_inc(S.r1, 1)
     v.wait_ge(S.r1, 1)
     v.tensor_copy(T.hib[:, :], T.rstd[:, :]).then_inc(S.h1, 1)
@@ -133,11 +159,12 @@ def rank_program(g, core, T, topo):
             sc.activation(blk, T.jj[:, :], AF.Copy, scale=T.w[:, c:c + 1]).then_inc(S["bd%d" % c], 1)
     for c in range(8):
         pe.wait_ge(S["bd%d" % c], 1)
-        h = 64 * (c % 2)
-        pe.matmul(bank[c // 2][:, h:h + 64], T.onesb[:, :], T.dg[:, 64 * c:64 * (c + 1)], True, True).then_inc(
+        o = 64 * (c % 2)
+        pe.matmul(bank[c // 2][:, o:o + 64], T.onesb[:, :], T.dg[:, 64 * c:64 * (c + 1)], True, True).then_inc(
             S["bm%d" % (c // 2)], 1)
 
-    v.wait_ge(S.ld, 16)
+    v.wait_ge(S.ld0, 16)
+    v.wait_ge(S.ld1, 16)
     for k in range(4):
         v.wait_ge(S["bm%d" % k], 2)
         v.tensor_tensor(T.ys[:, 128 * k:128 * (k + 1)], T.xs[:, 128 * k:128 * (k + 1)], bank[k][:, 0:128],
@@ -145,4 +172,4 @@ def rank_program(g, core, T, topo):
     sy.wait_ge(S.ym, 4)
     sy.dma_start(T.y[:, :], T.ys[:, :]).then_inc(S.st, 16)
     sy.wait_ge(S.st, 16)
-    g.wait_ge(S.sent, len(engines))
+    g.wait_ge(S.sent, 2 * len(engines))

@@ -24,7 +24,8 @@ SCRATCH = {
     "gg0": ("sbuf", [128, 128], "float32"),
     "gg1": ("sbuf", [128, 128], "float32"),
     "sd": ("sbuf", [128, 8], "float32"),
-    "rstd": ("sbuf", [128, 8], "float32"),
+    "u": ("sbuf", [128, 8], "float32"),
+    "rs": ("sbuf", [128, 8], "float32"),
     "hib": ("sbuf", [128, 8], "bfloat16"),
     "w": ("sbuf", [128, 8], "float32"),
     "dg": ("sbuf", [128, TK], "bfloat16"),
@@ -37,8 +38,9 @@ SCRATCH = {
     "b2": ("psum", [128, 512], "float32"),
     "b3": ("psum", [128, 512], "float32"),
 }
-SEMAPHORES = (["c_ones", "c_id", "c_set", "sent", "r1", "h1", "w1", "ym", "st"]
-              + [n + "%d" % h for h in range(2) for n in ("ld", "mm", "pc", "d1", "arr", "d2", "am", "ss")]
+SEMAPHORES = (["c_ones", "c_id", "c_set", "sent", "an0", "ss0", "ru0", "ru1", "s16", "s32", "r0s", "h0s", "w0", "w1",
+               "ym", "st"]
+              + [n + "%d" % h for h in range(2) for n in ("ld", "mm", "pc", "d1", "arr", "d2", "am")]
               + ["sq%d" % j for j in range(4)] + ["bd%d" % c for c in range(8)] + ["bm%d" % k for k in range(4)])
 
 
@@ -60,7 +62,6 @@ def rank_program(g, core, T, topo):
     v, sc, pe, sy = g.vector, g.scalar, g.tensor, g.sync
     bank = [T.b0, T.b1, T.b2, T.b3]
     ps_p = [T.ps_p0, T.ps_p1]
-    ps_a = [T.ps_a0, T.ps_a1]
     land = [T.land0, T.land1]
     gg = [T.gg0, T.gg1]
     end = [FIRST[h] + 128 * NB[h] for h in range(2)]
@@ -114,7 +115,8 @@ def rank_program(g, core, T, topo):
             pe.matmul(ps_p[h][:, j:j + 1], T.sqp[:, 128 * q:128 * (q + 1)], T.ones32[:, 0:1], True, True).then_inc(
                 S["mm%d" % h], 1)
         v.wait_ge(S["mm%d" % h], NB[h])
-        v.tensor_copy(T.part[:, 4 * h:4 * h + NB[h]], ps_p[h][:, 0:NB[h]]).then_inc(S["pc%d" % h], 1)
+        v.tensor_scalar(T.part[:, 4 * h:4 * h + NB[h]], ps_p[h][:, 0:NB[h]], 1.0 / D, EPS / N, AluOpType.mult,
+                        AluOpType.add).then_inc(S["pc%d" % h], 1)
         sy.wait_ge(S["pc%d" % h], 1)
         sy.dma_start(land[h][rank], T.part[:, 4 * h:4 * h + NB[h]]).then_inc(S["d1%d" % h], 16)
         g.wait_ge(S["d1%d" % h], 16)
@@ -128,36 +130,58 @@ def rank_program(g, core, T, topo):
             q.dma_start(gg[h][0:rows[h], 64 * i:64 * (i + 1)], land[h][:]).then_inc(S["d2%d" % h], 16)
 
     pe.wait_ge(S.c_set, n_set)
-    for h in range(2):
-        pe.wait_ge(S["d2%d" % h], 32)
-        pe.matmul(ps_a[h][:, 0:2 * NB[h]], gg[h][0:rows[h], :], T.sel[0:rows[h], col[h]:col[h] + 2 * NB[h]], True,
-                  True).then_inc(S["am%d" % h], 1)
+    pe.wait_ge(S.d20, 32)
+    pe.matmul(T.ps_a0[:, 0:2], T.gg0[0:rows[0], :], T.sel[0:rows[0], 0:2], True, True).then_inc(S.am0, 1)
+    pe.wait_ge(S.pc0, 1)
+    pe.matmul(T.ps_p0[:, 0:2], T.gg0[0:rows[0], :], T.sel[0:rows[0], 0:2], True, True).then_inc(S.an0, 1)
+    pe.wait_ge(S.d21, 32)
+    pe.matmul(T.ps_a1[:, 0:6], T.gg1[0:rows[1], :], T.sel[0:rows[1], 2:8], True, True).then_inc(S.am1, 1)
 
-    for h in range(2):
-        sc.wait_ge(S["am%d" % h], 1)
-        sc.activation(T.sd[:, col[h]:col[h] + 2 * NB[h]], ps_a[h][:, 0:2 * NB[h]], AF.Sqrt, bias=EPS,
-                      scale=1.0 / D).then_inc(S["ss%d" % h], 1)
+    sc.wait_ge(S.am0, 1)
+    sc.activation(T.sd[:, 0:2], T.ps_a0[:, 0:2], AF.Sqrt).then_inc(S.ss0, 1)
+    v.wait_ge(S.an0, 1)
+    v.reciprocal(T.u[:, 0:2], T.ps_p0[:, 0:2]).then_inc(S.ru0, 1)
+    v.wait_ge(S.am1, 1)
+    v.reciprocal(T.u[:, 2:8], T.ps_a1[:, 0:6]).then_inc(S.ru1, 1)
+    sc.wait_ge(S.ru1, 1)
+    sc.activation(T.hib[:, 2:8], T.u[:, 2:8], AF.Sqrt).then_inc(S.s16, 1)
+    sc.activation(T.rs[64:128, 2:8], T.u[64:128, 2:8], AF.Sqrt).then_inc(S.s32, 1)
+    sc.wait_ge(S.s16, 1)
+    sc.activation(T.w[0:64, 2:8], T.hib[0:64, 2:8], AF.Copy).then_inc(S.w1, 1)
     v.wait_ge(S.ss0, 1)
-    v.wait_ge(S.ss1, 1)
-    v.reciprocal(T.rstd[:, :], T.sd[:, :]).then_inc(S.r1, 1)
-    v.wait_ge(S.r1, 1)
-    v.tensor_copy(T.hib[:, :], T.rstd[:, :]).then_inc(S.h1, 1)
-    v.wait_ge(S.h1, 1)
-    v.tensor_tensor(T.w[64:128, :], T.rstd[64:128, :], T.hib[64:128, :], AluOpType.subtract).then_inc(S.w1, 1)
-    sc.wait_ge(S.h1, 1)
-    sc.activation(T.w[0:64, :], T.hib[0:64, :], AF.Copy).then_inc(S.w1, 1)
+    v.wait_ge(S.ru0, 1)
+    v.tensor_tensor(T.rs[:, 0:2], T.sd[:, 0:2], T.u[:, 0:2], AluOpType.mult).then_inc(S.r0s, 1)
+    v.wait_ge(S.s16, 1)
+    v.wait_ge(S.s32, 1)
+    v.tensor_tensor(T.w[64:128, 2:8], T.rs[64:128, 2:8], T.hib[64:128, 2:8], AluOpType.subtract).then_inc(S.w1, 1)
+    v.wait_ge(S.r0s, 1)
+    v.tensor_copy(T.hib[:, 0:2], T.rs[:, 0:2]).then_inc(S.h0s, 1)
+    v.wait_ge(S.h0s, 1)
+    v.tensor_tensor(T.w[64:128, 0:2], T.rs[64:128, 0:2], T.hib[64:128, 0:2], AluOpType.subtract).then_inc(S.w0, 1)
 
-    v.wait_ge(S.c_set, n_set)
-    v.wait_ge(S.w1, 2)
-    sc.wait_ge(S.c_set, n_set)
-    sc.wait_ge(S.w1, 2)
-    for c in range(8):
+    def build(c, on_vector):
         blk = T.dg[:, 64 * c:64 * (c + 1)]
-        if c % 2 == 0:
+        if on_vector:
             v.tensor_scalar(blk, T.jj[:, :], T.w[:, c:c + 1], None, AluOpType.mult).then_inc(S["bd%d" % c], 1)
         else:
             sc.activation(blk, T.jj[:, :], AF.Copy, scale=T.w[:, c:c + 1]).then_inc(S["bd%d" % c], 1)
-    for c in range(8):
+
+    sc.wait_ge(S.c_set, n_set)
+    sc.wait_ge(S.w1, 2)
+    build(2, False)
+    build(3, False)
+    sc.wait_ge(S.h0s, 1)
+    sc.activation(T.w[0:64, 0:2], T.hib[0:64, 0:2], AF.Copy).then_inc(S.w0, 1)
+    build(4, False)
+    build(5, False)
+    v.wait_ge(S.c_set, n_set)
+    v.wait_ge(S.w1, 2)
+    build(6, True)
+    build(7, True)
+    v.wait_ge(S.w0, 2)
+    build(0, True)
+    build(1, True)
+    for c in (2, 3, 6, 7, 4, 5, 0, 1):
         pe.wait_ge(S["bd%d" % c], 1)
         o = 64 * (c % 2)
         pe.matmul(bank[c // 2][:, o:o + 64], T.onesb[:, :], T.dg[:, 64 * c:64 * (c + 1)], True, True).then_inc(
@@ -165,7 +189,7 @@ def rank_program(g, core, T, topo):
 
     v.wait_ge(S.ld0, 16)
     v.wait_ge(S.ld1, 16)
-    for k in range(4):
+    for k in (1, 3, 2, 0):
         v.wait_ge(S["bm%d" % k], 2)
         v.tensor_tensor(T.ys[:, 128 * k:128 * (k + 1)], T.xs[:, 128 * k:128 * (k + 1)], bank[k][:, 0:128],
                         AluOpType.mult).then_inc(S.ym, 1)

@@ -25,7 +25,6 @@ SCRATCH = {
     "gg1": ("sbuf", [128, 128], "float32"),
     "sd": ("sbuf", [128, 8], "float32"),
     "u": ("sbuf", [128, 8], "float32"),
-    "rs": ("sbuf", [128, 8], "float32"),
     "hib": ("sbuf", [128, 8], "bfloat16"),
     "w": ("sbuf", [128, 8], "float32"),
     "dg": ("sbuf", [128, TK], "bfloat16"),
@@ -38,8 +37,7 @@ SCRATCH = {
     "b2": ("psum", [128, 512], "float32"),
     "b3": ("psum", [128, 512], "float32"),
 }
-SEMAPHORES = (["c_ones", "c_id", "c_set", "sent", "an0", "ss0", "ru0", "ru1", "s16", "s32", "r0s", "h0s", "w0", "w1",
-               "ym", "st"]
+SEMAPHORES = (["c_ones", "c_id", "c_set", "sent", "an0", "ss0", "ru0", "ru1", "s16", "s32", "r0s", "w1", "ym", "st"]
               + [n + "%d" % h for h in range(2) for n in ("ld", "mm", "pc", "d1", "arr", "d2", "am")]
               + ["sq%d" % j for j in range(4)] + ["bd%d" % c for c in range(8)] + ["bm%d" % k for k in range(4)])
 
@@ -51,6 +49,10 @@ def _hops(topo, a, b):
     if topo.mates(ca, cb) or topo.same_plane(ca, cb):
         return 1
     return 2
+
+
+def _bits(mask):
+    return [b for b in range(16) if (mask >> b) & 1]
 
 
 def rank_program(g, core, T, topo):
@@ -84,18 +86,28 @@ def rank_program(g, core, T, topo):
     n_set = 10
 
     others = [c for c in T.cores if c != core]
-    common = 0xFFFF
+    common = topo.mask(core, others[0])
     for c in others:
         assert topo.may_write(core, c)
         common &= topo.mask(core, c)
-    bits = [b for b in range(16) if (common >> b) & 1]
-    engines = bits[::2][:NENG]
+    engines = _bits(common)[::2][:NENG]
     others.sort(key=lambda c: -_hops(topo, core, c))
+    near = [c for c in others if _hops(topo, core, c) == 0]
+    spare = []
+    if near:
+        free = topo.mask(core, near[0])
+        for c in near:
+            free &= topo.mask(core, c)
+        spare = _bits(free & ~common)[::2][:NENG]
+    direct = near if len(spare) == NENG else []
+    smask = 0
+    for b in spare:
+        smask |= 1 << b
 
-    def gather_call(slot, sem):
+    def gather_call(slot, sem, dests):
         transfers = []
         for e, b in enumerate(engines):
-            mine = others[e::len(engines)]
+            mine = dests[e::len(engines)]
             ids = []
             for c in mine:
                 rid, pid, _se = topo.addr(c)
@@ -119,14 +131,20 @@ def rank_program(g, core, T, topo):
                         AluOpType.add).then_inc(S["pc%d" % h], 1)
         sy.wait_ge(S["pc%d" % h], 1)
         sy.dma_start(land[h][rank], T.part[:, 4 * h:4 * h + NB[h]]).then_inc(S["d1%d" % h], 16)
+        if h == 0 and direct:
+            g.wait_ge(S.pc0, 1)
+            for c in direct:
+                rid, pid, _se = topo.addr(c)
+                g.remote_dma(land[0][rank], T.part[:, 0:1], S.arr0, S.sent, pid, rid, smask)
         g.wait_ge(S["d1%d" % h], 16)
-        gather_call(land[h][rank], S["arr%d" % h])
+        gather_call(land[h][rank], S["arr%d" % h], [c for c in others if h == 1 or c not in direct])
+    n_arr = [N - 1 + (NENG - 1) * len(direct), N - 1]
 
     for h, queues in ((0, (sy, sc)), (1, (sy, sy))):
         for i, q in enumerate(queues):
             if i == 0 or q is not queues[0]:
                 q.wait_ge(S["d1%d" % h], 16)
-                q.wait_ge(S["arr%d" % h], N - 1)
+                q.wait_ge(S["arr%d" % h], n_arr[h])
             q.dma_start(gg[h][0:rows[h], 64 * i:64 * (i + 1)], land[h][:]).then_inc(S["d2%d" % h], 16)
 
     pe.wait_ge(S.c_set, n_set)
@@ -144,20 +162,16 @@ def rank_program(g, core, T, topo):
     v.wait_ge(S.am1, 1)
     v.reciprocal(T.u[:, 2:8], T.ps_a1[:, 0:6]).then_inc(S.ru1, 1)
     sc.wait_ge(S.ru1, 1)
-    sc.activation(T.hib[:, 2:8], T.u[:, 2:8], AF.Sqrt).then_inc(S.s16, 1)
-    sc.activation(T.rs[64:128, 2:8], T.u[64:128, 2:8], AF.Sqrt).then_inc(S.s32, 1)
-    sc.wait_ge(S.s16, 1)
-    sc.activation(T.w[0:64, 2:8], T.hib[0:64, 2:8], AF.Copy).then_inc(S.w1, 1)
+    sc.activation(T.hib[64:128, 2:8], T.u[64:128, 2:8], AF.Sqrt).then_inc(S.s16, 1)
+    sc.activation(T.w[:, 2:8], T.u[:, 2:8], AF.Sqrt).then_inc(S.s32, 1)
     v.wait_ge(S.ss0, 1)
     v.wait_ge(S.ru0, 1)
-    v.tensor_tensor(T.rs[:, 0:2], T.sd[:, 0:2], T.u[:, 0:2], AluOpType.mult).then_inc(S.r0s, 1)
+    v.tensor_tensor(T.w[:, 0:2], T.sd[:, 0:2], T.u[:, 0:2], AluOpType.mult).then_inc(S.r0s, 1)
+    v.tensor_tensor(T.hib[64:128, 0:2], T.sd[64:128, 0:2], T.u[64:128, 0:2], AluOpType.mult).then_inc(S.r0s, 1)
+    v.wait_ge(S.r0s, 2)
     v.wait_ge(S.s16, 1)
     v.wait_ge(S.s32, 1)
-    v.tensor_tensor(T.w[64:128, 2:8], T.rs[64:128, 2:8], T.hib[64:128, 2:8], AluOpType.subtract).then_inc(S.w1, 1)
-    v.wait_ge(S.r0s, 1)
-    v.tensor_copy(T.hib[:, 0:2], T.rs[:, 0:2]).then_inc(S.h0s, 1)
-    v.wait_ge(S.h0s, 1)
-    v.tensor_tensor(T.w[64:128, 0:2], T.rs[64:128, 0:2], T.hib[64:128, 0:2], AluOpType.subtract).then_inc(S.w0, 1)
+    v.tensor_tensor(T.w[64:128, :], T.w[64:128, :], T.hib[64:128, :], AluOpType.subtract).then_inc(S.w1, 1)
 
     def build(c, on_vector):
         blk = T.dg[:, 64 * c:64 * (c + 1)]
@@ -167,21 +181,16 @@ def rank_program(g, core, T, topo):
             sc.activation(blk, T.jj[:, :], AF.Copy, scale=T.w[:, c:c + 1]).then_inc(S["bd%d" % c], 1)
 
     sc.wait_ge(S.c_set, n_set)
-    sc.wait_ge(S.w1, 2)
-    build(2, False)
-    build(3, False)
-    sc.wait_ge(S.h0s, 1)
-    sc.activation(T.w[0:64, 0:2], T.hib[0:64, 0:2], AF.Copy).then_inc(S.w0, 1)
-    build(4, False)
-    build(5, False)
+    sc.wait_ge(S.s32, 1)
+    sc.wait_ge(S.r0s, 2)
+    sc.wait_ge(S.w1, 1)
+    for c in (0, 1, 4, 5, 7):
+        build(c, False)
     v.wait_ge(S.c_set, n_set)
-    v.wait_ge(S.w1, 2)
-    build(6, True)
-    build(7, True)
-    v.wait_ge(S.w0, 2)
-    build(0, True)
-    build(1, True)
-    for c in (2, 3, 6, 7, 4, 5, 0, 1):
+    v.wait_ge(S.w1, 1)
+    for c in (2, 3, 6):
+        build(c, True)
+    for c in (0, 2, 1, 3, 4, 6, 5, 7):
         pe.wait_ge(S["bd%d" % c], 1)
         o = 64 * (c % 2)
         pe.matmul(bank[c // 2][:, o:o + 64], T.onesb[:, :], T.dg[:, 64 * c:64 * (c + 1)], True, True).then_inc(
@@ -189,11 +198,11 @@ def rank_program(g, core, T, topo):
 
     v.wait_ge(S.ld0, 16)
     v.wait_ge(S.ld1, 16)
-    for k in (1, 3, 2, 0):
+    for k in (0, 1, 2, 3):
         v.wait_ge(S["bm%d" % k], 2)
         v.tensor_tensor(T.ys[:, 128 * k:128 * (k + 1)], T.xs[:, 128 * k:128 * (k + 1)], bank[k][:, 0:128],
                         AluOpType.mult).then_inc(S.ym, 1)
     sy.wait_ge(S.ym, 4)
     sy.dma_start(T.y[:, :], T.ys[:, :]).then_inc(S.st, 16)
     sy.wait_ge(S.st, 16)
-    g.wait_ge(S.sent, 2 * len(engines))
+    g.wait_ge(S.sent, 2 * len(engines) + NENG * len(direct))

from concourse.bass import DstId, RemoteDMATransfer
from concourse.mybir import AluOpType, AxisListType, ActivationFunctionType

N = 10
TK = 512
D = 128 * N
EPS = 0.01
NENG = 4
FIRST = (0, 128)
NB = (1, 3)

SCRATCH = {
    "xs": ("sbuf", [128, TK], "float32"),
    "sqp": ("sbuf", [128, TK], "float32"),
    "ys": ("sbuf", [128, TK], "float32"),
    "ones32": ("sbuf", [128, 128], "float32"),
    "ident": ("sbuf", [128, 128], "float32"),
    "onesb": ("sbuf", [128, 128], "bfloat16"),
    "jj": ("sbuf", [128, 64], "bfloat16"),
    "sel": ("sbuf", [128, 8], "float32"),
    "part": ("sbuf", [128, 8], "float32"),
    "land0": ("dram", [N, 128, NB[0]], "float32"),
    "land1": ("dram", [N, 128, NB[1]], "float32"),
    "gg0": ("sbuf", [128, 128], "float32"),
    "gg1": ("sbuf", [128, 128], "float32"),
    "sd": ("sbuf", [128, 8], "float32"),
    "u": ("sbuf", [128, 8], "float32"),
    "hib": ("sbuf", [128, 8], "bfloat16"),
    "w": ("sbuf", [128, 8], "float32"),
    "dg": ("sbuf", [128, TK], "bfloat16"),
    "ps_p0": ("psum", [128, 512], "float32"),
    "ps_p1": ("psum", [128, 512], "float32"),
    "ps_a0": ("psum", [128, 512], "float32"),
    "ps_a1": ("psum", [128, 512], "float32"),
    "b0": ("psum", [128, 512], "float32"),
    "b1": ("psum", [128, 512], "float32"),
    "b2": ("psum", [128, 512], "float32"),
    "b3": ("psum", [128, 512], "float32"),
}
SEMAPHORES = (["c_ones", "c_id", "c_set", "sent", "an0", "ss0", "ru0", "ru1", "s16", "s32", "r0s", "w1", "ym", "st"]
              + [n + "%d" % h for h in range(2) for n in ("ld", "mm", "pc", "d1", "arr", "d2", "am")]
              + ["sq%d" % j for j in range(4)] + ["bd%d" % c for c in range(8)] + ["bm%d" % k for k in range(4)])


def _hops(topo, a, b):
    ca, cb = topo.chip(a), topo.chip(b)
    if ca == cb:
        return 0
    if topo.mates(ca, cb) or topo.same_plane(ca, cb):
        return 1
    return 2


def _bits(mask):
    return [b for b in range(16) if (mask >> b) & 1]


def rank_program(g, core, T, topo):
    rank = T.rank_of(core)
    if rank is None:
        return
    S = T.sem
    AF = ActivationFunctionType
    v, sc, pe, sy = g.vector, g.scalar, g.tensor, g.sync
    bank = [T.b0, T.b1, T.b2, T.b3]
    ps_p = [T.ps_p0, T.ps_p1]
    land = [T.land0, T.land1]
    gg = [T.gg0, T.gg1]
    end = [FIRST[h] + 128 * NB[h] for h in range(2)]
    col = [FIRST[h] // 64 for h in range(2)]
    rows = [2 * NB[h] * N for h in range(2)]

    for h in range(2):
        sy.dma_start(T.xs[:, FIRST[h]:end[h]], T.x[:, FIRST[h]:end[h]]).then_inc(S["ld%d" % h], 16)

    v.memset(T.ones32[:, :], 1.0).then_inc(S.c_ones, 1)
    v.memset(T.onesb[:, :], 1.0).then_inc(S.c_set, 1)
    g.wait_ge(S.c_ones, 1)
    g.affine_select(T.ident[:, :], T.ones32[:, :], [[-1, 128]], AluOpType.is_equal, 0.0, 0, 1).then_inc(S.c_id, 1)
    v.wait_ge(S.c_id, 1)
    v.tensor_tensor(T.jj[:, :], T.ident[:, 0:64], T.ident[:, 64:128], AluOpType.add).then_inc(S.c_set, 1)
    for h in range(2):
        for b in range(2 * NB[h]):
            v.tensor_reduce(T.sel[:, col[h] + b:col[h] + b + 1], T.ident[:, b:rows[h]:2 * NB[h]], AxisListType.X,
                            AluOpType.add).then_inc(S.c_set, 1)
    n_set = 10

    others = [c for c in T.cores if c != core]
    common = topo.mask(core, others[0])
    for c in others:
        assert topo.may_write(core, c)
        common &= topo.mask(core, c)
    engines = _bits(common)[::2][:NENG]
    others.sort(key=lambda c: -_hops(topo, core, c))
    near = [c for c in others if _hops(topo, core, c) == 0]
    spare = []
    if near:
        free = topo.mask(core, near[0])
        for c in near:
            free &= topo.mask(core, c)
        spare = _bits(free & ~common)[::2][:NENG]
    direct = near if len(spare) == NENG else []
    smask = 0
    for b in spare:
        smask |= 1 << b

    def gather_call(slot, sem, dests):
        transfers = []
        for e, b in enumerate(engines):
            mine = dests[e::len(engines)]
            ids = []
            for c in mine:
                rid, pid, _se = topo.addr(c)
                ids.append(DstId(rid=rid, pnc=pid))
            transfers.append(RemoteDMATransfer(dst_ids=ids, dma_engine_mask=1 << b, remote_sem=sem,
                                               srcs=[slot], dsts=[slot for _c in mine]))
        g.remote_dma_fused(transfers, local_sem=S.sent)

    pe.wait_ge(S.c_ones, 1)
    for h in range(2):
        sc.wait_ge(S["ld%d" % h], 16)
        for j in range(NB[h]):
            q = FIRST[h] // 128 + j
            sc.activation(T.sqp[:, 128 * q:128 * (q + 1)], T.xs[:, FIRST[h] + j:end[h]:NB[h]], AF.Square).then_inc(
                S["sq%d" % q], 1)
            pe.wait_ge(S["sq%d" % q], 1)
            pe.matmul(ps_p[h][:, j:j + 1], T.sqp[:, 128 * q:128 * (q + 1)], T.ones32[:, 0:1], True, True).then_inc(
                S["mm%d" % h], 1)
        v.wait_ge(S["mm%d" % h], NB[h])
        v.tensor_scalar(T.part[:, 4 * h:4 * h + NB[h]], ps_p[h][:, 0:NB[h]], 1.0 / D, EPS / N, AluOpType.mult,
                        AluOpType.add).then_inc(S["pc%d" % h], 1)
        sy.wait_ge(S["pc%d" % h], 1)
        sy.dma_start(land[h][rank], T.part[:, 4 * h:4 * h + NB[h]]).then_inc(S["d1%d" % h], 16)
        if h == 0 and direct:
            g.wait_ge(S.pc0, 1)
            for c in direct:
                rid, pid, _se = topo.addr(c)
                g.remote_dma(land[0][rank], T.part[:, 0:1], S.arr0, S.sent, pid, rid, smask)
        g.wait_ge(S["d1%d" % h], 16)
        gather_call(land[h][rank], S["arr%d" % h], [c for c in others if h == 1 or c not in direct])
    n_arr = [N - 1 + (NENG - 1) * len(direct), N - 1]

    for h, queues in ((0, (sy, sc)), (1, (sy, sy))):
        for i, q in enumerate(queues):
            if i == 0 or q is not queues[0]:
                q.wait_ge(S["d1%d" % h], 16)
                q.wait_ge(S["arr%d" % h], n_arr[h])
            q.dma_start(gg[h][0:rows[h], 64 * i:64 * (i + 1)], land[h][:]).then_inc(S["d2%d" % h], 16)

    pe.wait_ge(S.c_set, n_set)
    pe.wait_ge(S.d20, 32)
    pe.matmul(T.ps_a0[:, 0:2], T.gg0[0:rows[0], :], T.sel[0:rows[0], 0:2], True, True).then_inc(S.am0, 1)
    pe.wait_ge(S.pc0, 1)
    pe.matmul(T.ps_p0[:, 0:2], T.gg0[0:rows[0], :], T.sel[0:rows[0], 0:2], True, True).then_inc(S.an0, 1)
    pe.wait_ge(S.d21, 32)
    pe.matmul(T.ps_a1[:, 0:6], T.gg1[0:rows[1], :], T.sel[0:rows[1], 2:8], True, True).then_inc(S.am1, 1)

    sc.wait_ge(S.am0, 1)
    sc.activation(T.sd[:, 0:2], T.ps_a0[:, 0:2], AF.Sqrt).then_inc(S.ss0, 1)
    v.wait_ge(S.an0, 1)
    v.reciprocal(T.u[:, 0:2], T.ps_p0[:, 0:2]).then_inc(S.ru0, 1)
    v.wait_ge(S.am1, 1)
    v.reciprocal(T.u[:, 2:8], T.ps_a1[:, 0:6]).then_inc(S.ru1, 1)
    sc.wait_ge(S.ru1, 1)
    sc.activation(T.hib[64:128, 2:8], T.u[64:128, 2:8], AF.Sqrt).then_inc(S.s16, 1)
    sc.activation(T.w[:, 2:8], T.u[:, 2:8], AF.Sqrt).then_inc(S.s32, 1)
    v.wait_ge(S.ss0, 1)
    v.wait_ge(S.ru0, 1)
    v.tensor_tensor(T.w[:, 0:2], T.sd[:, 0:2], T.u[:, 0:2], AluOpType.mult).then_inc(S.r0s, 1)
    v.tensor_tensor(T.hib[64:128, 0:2], T.sd[64:128, 0:2], T.u[64:128, 0:2], AluOpType.mult).then_inc(S.r0s, 1)
    v.wait_ge(S.r0s, 2)
    v.wait_ge(S.s16, 1)
    v.wait_ge(S.s32, 1)
    v.tensor_tensor(T.w[64:128, :], T.w[64:128, :], T.hib[64:128, :], AluOpType.subtract).then_inc(S.w1, 1)

    def build(c, on_vector):
        blk = T.dg[:, 64 * c:64 * (c + 1)]
        if on_vector:
            v.tensor_scalar(blk, T.jj[:, :], T.w[:, c:c + 1], None, AluOpType.mult).then_inc(S["bd%d" % c], 1)
        else:
            sc.activation(blk, T.jj[:, :], AF.Copy, scale=T.w[:, c:c + 1]).then_inc(S["bd%d" % c], 1)

    sc.wait_ge(S.c_set, n_set)
    sc.wait_ge(S.s32, 1)
    sc.wait_ge(S.r0s, 2)
    sc.wait_ge(S.w1, 1)
    for c in (0, 1, 4, 5, 7):
        build(c, False)
    v.wait_ge(S.c_set, n_set)
    v.wait_ge(S.w1, 1)
    for c in (2, 3, 6):
        build(c, True)
    for c in (0, 2, 1, 3, 4, 6, 5, 7):
        pe.wait_ge(S["bd%d" % c], 1)
        o = 64 * (c % 2)
        pe.matmul(bank[c // 2][:, o:o + 64], T.onesb[:, :], T.dg[:, 64 * c:64 * (c + 1)], True, True).then_inc(
            S["bm%d" % (c // 2)], 1)

    v.wait_ge(S.ld0, 16)
    v.wait_ge(S.ld1, 16)
    for k in (0, 1, 2, 3):
        v.wait_ge(S["bm%d" % k], 2)
        v.tensor_tensor(T.ys[:, 128 * k:128 * (k + 1)], T.xs[:, 128 * k:128 * (k + 1)], bank[k][:, 0:128],
                        AluOpType.mult).then_inc(S.ym, 1)
    sy.wait_ge(S.ym, 4)
    sy.dma_start(T.y[:, :], T.ys[:, :]).then_inc(S.st, 16)
    sy.wait_ge(S.st, 16)
    g.wait_ge(S.sent, 2 * len(engines) + NENG * len(direct))
